import numpy as np
import ml_dtypes


def mxq(x, axis, fmt="e4m3"):
    dtype, down = {"e4m3": (ml_dtypes.float8_e4m3fn, 7), "e5m2": (ml_dtypes.float8_e5m2, 14)}[fmt]
    v = np.moveaxis(np.asarray(x, np.float32).astype(ml_dtypes.bfloat16).astype(np.float64), axis, -1)
    blocks = v.reshape(v.shape[:-1] + (-1, 32))
    amax = np.abs(blocks).max(-1, keepdims=True)
    byte = np.maximum(np.where(amax > 0, np.frexp(amax)[1] - 1 + 127, 0) - down, 1)
    scale = np.exp2(byte - 127.0)
    codes = (blocks / scale).astype(np.float32).astype(dtype).astype(np.float64)
    return np.moveaxis((codes * scale).reshape(v.shape), -1, axis)


WIDE = False


def mx_kscale(k):
    if not WIDE:
        return np.ones(k)
    levels = np.array([10, -10, 5, -5, 0])
    if k % 512:
        return np.exp2(np.random.permutation(np.resize(levels, k // 32))).repeat(32)
    a = np.empty((k // 512, 16))
    for p in range(k // 512):
        a[p, :8] = np.random.permutation(np.resize(levels, 8))
        for g in range(8):
            far = levels[np.abs(levels - a[p, g]) >= 10]
            a[p, g + 8] = far[np.random.randint(len(far))]
    return np.exp2(a.ravel()).repeat(32)


def f64(x):
    return np.asarray(x).astype(np.float64)


def striped(idx):
    return np.tile(np.asarray(idx).reshape(-1, 16).T, (8, 1)).astype(np.uint16)


def unstriped(offs):
    return offs[:16].T.reshape(-1).astype(np.int64)


E2M1 = np.array([0.0, 0.5, 1.0, 1.5, 2.0, 3.0, 4.0, 6.0, -0.0, -0.5, -1.0, -1.5, -2.0, -3.0, -4.0, -6.0])


def pack_weight(w, fmt):
    k, n = w.shape
    w = f64(np.asarray(w, np.float32).astype(ml_dtypes.bfloat16)).reshape(k // 32, 32, n)
    amax = np.abs(w).max(1)
    if fmt == "e4m3":
        byte = np.frexp(amax)[1] - 1 + 127 - 7
    else:
        mant, ex = np.frexp(amax / 6.0)
        byte = np.where(mant > 0.5, ex, ex - 1) + 127
    byte = np.clip(np.where(amax > 0, byte, 1), 1, 254)
    scaled = (w * np.exp2(127.0 - byte)[:, None, :]).reshape(k, n).astype(np.float32)
    by_word = np.ascontiguousarray(scaled.reshape(k // 512, 128, 4, n).transpose(0, 1, 3, 2))
    if fmt == "e4m3":
        words = by_word.astype(ml_dtypes.float8_e4m3fn).view(np.uint8)
    else:
        c = by_word.astype(ml_dtypes.float4_e2m1fn).view(np.uint8) & 0xF
        words = (c[..., 0::2] | (c[..., 1::2] << 4)).reshape(k // 512, 128, 2 * n)
    return np.ascontiguousarray(words), np.ascontiguousarray(byte.astype(np.uint8).reshape(k // 512, 16, n))


def unpack_weight(words, scales, fmt):
    g, _, n = scales.shape
    words = np.ascontiguousarray(words).reshape(g, 128, n, -1)
    if fmt == "e4m3":
        vals = words.view(ml_dtypes.float8_e4m3fn).astype(np.float64)
    else:
        nib = np.empty((g, 128, n, 4), np.uint8)
        nib[..., 0::2] = words & 0xF
        nib[..., 1::2] = words >> 4
        vals = E2M1[nib]
    vals = vals * np.repeat(np.exp2(scales.astype(np.float64) - 127.0), 8, axis=1)[..., None]
    return vals.transpose(0, 1, 3, 2).reshape(g * 512, n)


def silu(v):
    return v / (1.0 + np.exp(-v))


B, N, T, D, NQ = 1, 512, 2048, 512, 512
DV = 512


def sgn(shape):
    return np.random.uniform(0.5, 2.0, shape) * np.where(np.random.standard_normal(shape) < 0, -1.0, 1.0)


def setup_inputs():
    n = np.random.standard_normal
    pages = np.random.permutation(T // 64)[:B * N // 64]
    idx = (pages[:, None] * 64 + np.arange(64)[None, :]).reshape(-1)
    s = mx_kscale(D)[:, None]
    u = mx_kscale(N)
    ut = np.ones(T)
    ut[idx] = u
    kp = pack_weight(n((D, T)) / s, "e4m3")
    return {
        "qT": (n((B, D, NQ)) * s * (1.00 / np.sqrt(D))).astype(np.float32),
        "k_words": kp[0],
        "k_scales": kp[1],
        "vT": (n((DV, T)) / ut).astype(np.float32),
        "us": (sgn((B, N, 1)) * u[:, None]).astype(np.float32),
        "rw": (np.random.uniform(0.1, 1.0, (B, NQ, 1))).astype(np.float32),
        "offs": striped(idx),
    }


def reference(qT, k_words, k_scales, vT, us, rw, offs):
    idx = unstriped(offs)
    pick = lambda x, which: x[:, which].reshape(x.shape[0], B, -1).transpose(1, 0, 2)
    k = unpack_weight(k_words, k_scales, "e4m3")
    kg = pick(k, idx)
    qq = mxq(f64(qT), 1, "e4m3")
    a = kg.transpose(0, 2, 1) @ qq
    y = silu(a) * f64(us)
    wq = mxq(y, 1, "e4m3")
    o = wq.transpose(0, 2, 1) @ mxq(pick(f64(vT), idx).transpose(0, 2, 1), 1, "e4m3")
    r_ = o * f64(rw)
    return r_

@@ -1,0 +1,170 @@
+from contextlib import ExitStack
+
+import concourse.mybir as mybir
+from concourse.masks import make_identity
+
+D, NQ, T, SLOTS, DV = 512, 512, 2048, 512, 512
+FLOPS = 2 * SLOTS * NQ * D + 2 * NQ * SLOTS * DV
+
+F32 = mybir.dt.float32
+BF16 = mybir.dt.bfloat16
+I32 = mybir.dt.int32
+U32 = mybir.dt.uint32
+U16 = mybir.dt.uint16
+U8 = mybir.dt.uint8
+FP8X4 = mybir.dt.float8_e4m3fn_x4
+ACT = mybir.ActivationFunctionType
+MULT = mybir.AluOpType.mult
+
+P = 128
+PACK = 4
+CH = NQ // P
+EB = DV // P
+HALF = NQ // 2
+
+
+def tile_attend_mlp_silu_kernel(tc, qT, k_words, k_scales, vT, us, rw, offs, out):
+    nc = tc.nc
+    with ExitStack() as ctx:
+        keep = ctx.enter_context(tc.tile_pool(name="keep", bufs=1))
+        psum = ctx.enter_context(tc.psum_pool(name="psum", bufs=1))
+
+        offsets = keep.tile([P, SLOTS // 16], U16, name="offsets")
+        nc.sync.dma_start(offsets[:], offs)
+
+        ks_pool = keep.tile([P, T], U8, name="ks_pool", align_bytes=64)
+        nc.vector.memset(ks_pool[:].bitcast(I32), 0)
+        kw_pool = keep.tile([P, T], I32, name="kw_pool", align_bytes=64)
+        nc.sync.dma_start(kw_pool[:], k_words[0].rearrange("p n t -> p (n t)").bitcast(I32))
+        for quad in range(4):
+            nc.sync.dma_start(
+                ks_pool[32 * quad : 32 * quad + 4, :].bitcast(I32),
+                k_scales[0, 4 * quad : 4 * quad + 4, :].bitcast(I32),
+            )
+        q_rows = qT[0].rearrange("(p j) q -> p j q", j=PACK)
+        q_raw = []
+        for h in range(2):
+            t = keep.tile([P, PACK, HALF], F32, name=f"q_raw{h}")
+            nc.sync.dma_start(t[:], q_rows[:, :, h * HALF : (h + 1) * HALF])
+            q_raw.append(t)
+        v_pool = []
+        for j in range(EB):
+            t = keep.tile([P, T], F32, name=f"v_pool{j}", align_bytes=64)
+            nc.sync.dma_start(t[:], vT[j * P : (j + 1) * P, :])
+            v_pool.append(t)
+
+        us_cols = keep.tile([P, PACK], F32, name="us_cols")
+        nc.gpsimd.dma_start(us_cols[:], us[0].rearrange("(p t) o -> p (t o)", t=PACK))
+        rw_rows = keep.tile([P, P], F32, name="rw_rows")
+        nc.gpsimd.memset(rw_rows[:], 0.0)
+        nc.gpsimd.dma_start(rw_rows[0:CH, :], rw[0].rearrange("(c p) o -> c (p o)", p=P))
+        ident = keep.tile([P, P], F32, name="ident")
+        make_identity(nc, ident[:])
+
+        warm_in = keep.tile([P, 1], F32, name="warm_in")
+        warm_out = keep.tile([P, 1], F32, name="warm_out")
+        nc.vector.memset(warm_in[:], 0.0)
+        nc.scalar.activation(warm_out[:], warm_in[:], ACT.Silu)
+
+        rw_turned = psum.tile([P, 2, P], F32, name="rw_turned", tag="turn", bufs=2)
+        nc.tensor.transpose(rw_turned[:, 0, :], rw_rows[:], ident[:])
+        rw_cols = keep.tile([P, CH], F32, name="rw_cols")
+        nc.scalar.copy(rw_cols[:], rw_turned[:, 0, 0:CH])
+
+        ks_listed = keep.tile([P, SLOTS], U8, name="ks_listed", align_bytes=64)
+        nc.vector.tensor_copy(ks_listed[:], ks_pool[:].indirect(offsets[:]))
+        k_codes = keep.tile([P, PACK, P], U32, name="k_codes", align_bytes=64)
+        nc.vector.tensor_copy(
+            k_codes[:].rearrange("p t s -> p s t"), kw_pool[:].bitcast(U32).indirect(offsets[:])
+        )
+        k_scale = keep.tile([P, PACK, P], U8, name="k_scale", align_bytes=64)
+        nc.vector.tensor_copy(k_scale[:], ks_listed[:].rearrange("p (s t) -> p t s", t=PACK))
+
+        q_codes, q_scale = [], []
+        for h in range(2):
+            grouped = keep.tile([P, HALF, PACK], BF16, name=f"q_grouped{h}", align_bytes=64)
+            dst = grouped[:].rearrange("p (c i) t -> p c t i", i=4)
+            src = q_raw[h][:].rearrange("p t (c i) -> p c t i", i=4)
+            if h == 0:
+                nc.vector.tensor_copy(dst, src)
+            else:
+                nc.scalar.copy(dst, src)
+            codes = keep.tile([P, HALF], U32, name=f"q_codes{h}", align_bytes=64)
+            scale = keep.tile([P, HALF], U8, name=f"q_scale{h}", align_bytes=64)
+            nc.vector.quantize_mx(
+                out=codes[:].bitcast(FP8X4), scales=scale[:], in_=grouped[:].rearrange("p w t -> p (w t)")
+            )
+            q_codes.append(codes)
+            q_scale.append(scale)
+
+        us_wide = us_cols[:].unsqueeze(1).to_broadcast([P, P, PACK])
+        y_codes, y_scale, y_grouped = [], [], []
+
+        def quantise_y(c):
+            codes = keep.tile([P, P], U32, name=f"y_codes{c}", align_bytes=64)
+            scale = keep.tile([P, P], U8, name=f"y_scale{c}", align_bytes=64)
+            nc.vector.quantize_mx(
+                out=codes[:].bitcast(FP8X4), scales=scale[:], in_=y_grouped[c][:].rearrange("p w t -> p (w t)")
+            )
+            y_codes.append(codes)
+            y_scale.append(scale)
+
+        for c in range(CH):
+            h, cols = c // 2, slice((c % 2) * P, (c % 2 + 1) * P)
+            a = psum.tile([P, PACK, P], F32, name="a", tag="a", bufs=2)
+            for t in range(PACK):
+                nc.tensor.matmul_mx(
+                    out=a[:, t, :],
+                    lhsT=k_codes[:, t, :].bitcast(FP8X4),
+                    lhsT_scale=k_scale[:, t, :],
+                    rhs=q_codes[h][:, cols].bitcast(FP8X4),
+                    rhs_scale=q_scale[h][:, cols],
+                    start=True,
+                    stop=True,
+                )
+            act = keep.tile([P, P, PACK], F32, name=f"act{c}")
+            nc.scalar.activation(act[:], a[:].rearrange("p t q -> p q t"), ACT.Silu)
+            grouped = keep.tile([P, P, PACK], BF16, name=f"y_grouped{c}", align_bytes=64)
+            nc.vector.tensor_tensor(grouped[:], act[:], us_wide, MULT)
+            y_grouped.append(grouped)
+            if c > 0:
+                quantise_y(c - 1)
+        quantise_y(CH - 1)
+
+        out_rows = out[0].rearrange("(c p) e -> p c e", p=P)
+        for j in range(EB):
+            listed = keep.tile([P, SLOTS], BF16, name=f"v_listed{j}", align_bytes=64)
+            nc.vector.tensor_copy(listed[:], v_pool[j][:].indirect(offsets[:]))
+            words = listed[:].bitcast(F32)
+            turned = psum.tile([P, 2, P], F32, name="v_turned", tag="turn", bufs=2)
+            for u in range(2):
+                nc.tensor.transpose(turned[:, u, :], words[:, u : 2 * P : 2], ident[:])
+            grouped = keep.tile([P, P, PACK], BF16, name=f"v_grouped{j}", align_bytes=64)
+            nc.scalar.copy(grouped[:].bitcast(F32), turned[:].rearrange("p u e -> p e u"))
+            codes = keep.tile([P, P], U32, name=f"v_codes{j}", align_bytes=64)
+            scale = keep.tile([P, P], U8, name=f"v_scale{j}", align_bytes=64)
+            nc.vector.quantize_mx(
+                out=codes[:].bitcast(FP8X4), scales=scale[:], in_=grouped[:].rearrange("p w t -> p (w t)")
+            )
+            parts = [range(CH)] if j < EB - 1 else [range(0, 2), range(2, CH)]
+            for part in parts:
+                n = len(part)
+                o = psum.tile([P, n, P], F32, name="o", tag="o", bufs=4)
+                res = keep.tile([P, n, P], F32, name=f"res{j}_{part.start}")
+                for i, c in enumerate(part):
+                    nc.tensor.matmul_mx(
+                        out=o[:, i, :],
+                        lhsT=y_codes[c][:].bitcast(FP8X4),
+                        lhsT_scale=y_scale[c][:],
+                        rhs=codes[:].bitcast(FP8X4),
+                        rhs_scale=scale[:],
+                        start=True,
+                        stop=True,
+                    )
+                if j == EB - 1 and part.start > 0:
+                    rw_wide = rw_cols[:, part.start : part.stop].unsqueeze(2).to_broadcast([P, n, P])
+                    nc.vector.tensor_tensor(res[:], o[:], rw_wide, MULT)
+                else:
+                    for i, c in enumerate(part):
+                        nc.scalar.activation(res[:, i, :], o[:, i, :], ACT.Copy, scale=rw_cols[:, c : c + 1])
+                nc.sync.dma_start(out_rows[:, part.start : part.stop, j * P : (j + 1) * P], res[:])

@@ -27,144 +27,152 @@ def tile_attend_mlp_silu_kernel(tc, qT, k_words, k_scales, vT, us, rw, offs, out
     nc = tc.nc
     with ExitStack() as ctx:
         keep = ctx.enter_context(tc.tile_pool(name="keep", bufs=1))
+        stage = ctx.enter_context(tc.tile_pool(name="stage", bufs=1))
         psum = ctx.enter_context(tc.psum_pool(name="psum", bufs=1))
+
+        def sb(shape, dtype, name, tag=None):
+            return keep.tile(shape, dtype, name=name, tag=tag or name, align_bytes=64)
+
+        def quantise(grouped, width, name, at=None):
+            if at is None:
+                codes = sb([P, width], U32, name + "_codes")
+            else:
+                codes = stage.tile([P, width], U32, name=name + "_codes", offset=at, align_bytes=64)
+            scale = sb([P, width], U8, name + "_scale")
+            nc.vector.quantize_mx(
+                out=codes[:].bitcast(FP8X4), scales=scale[:], in_=grouped[:].rearrange("p w t -> p (w t)")
+            )
+            return codes, scale
+
+        def product(dst, stat, stat_scale, mov, mov_scale):
+            nc.tensor.matmul_mx(
+                out=dst,
+                lhsT=stat.bitcast(FP8X4),
+                lhsT_scale=stat_scale,
+                rhs=mov.bitcast(FP8X4),
+                rhs_scale=mov_scale,
+                start=True,
+                stop=True,
+            )
 
         offsets = keep.tile([P, SLOTS // 16], U16, name="offsets")
         nc.sync.dma_start(offsets[:], offs)
-
-        ks_pool = keep.tile([P, T], U8, name="ks_pool", align_bytes=64)
-        nc.vector.memset(ks_pool[:].bitcast(I32), 0)
-        kw_pool = keep.tile([P, T], I32, name="kw_pool", align_bytes=64)
+        us_cols = sb([P, PACK], F32, "us_cols")
+        nc.scalar.dma_start(us_cols[:], us[0].rearrange("(p t) o -> p (t o)", t=PACK))
+        kw_pool = sb([P, T], I32, "kw_pool")
         nc.sync.dma_start(kw_pool[:], k_words[0].rearrange("p n t -> p (n t)").bitcast(I32))
+        ks_pool = sb([P, T], U8, "ks_pool")
+        nc.gpsimd.memset(ks_pool[:].bitcast(I32), 0)
         for quad in range(4):
             nc.sync.dma_start(
                 ks_pool[32 * quad : 32 * quad + 4, :].bitcast(I32),
                 k_scales[0, 4 * quad : 4 * quad + 4, :].bitcast(I32),
             )
+        warm_in = stage.tile([P, (1 + EB) * T], F32, name="warm_in", offset=0)
+        warm_out = sb([P, 1], F32, "warm_out")
+        nc.gpsimd.memset(warm_in[:, 0:1], 0.0)
+        nc.scalar.activation(warm_out[:], warm_in[:, 0:1], ACT.Silu)
+
         q_rows = qT[0].rearrange("(p j) q -> p j q", j=PACK)
         q_raw = []
         for h in range(2):
-            t = keep.tile([P, PACK, HALF], F32, name=f"q_raw{h}")
+            t = stage.tile([P, PACK, HALF], F32, name=f"q_raw{h}", offset=h * T * 2)
             nc.sync.dma_start(t[:], q_rows[:, :, h * HALF : (h + 1) * HALF])
             q_raw.append(t)
+
         v_pool = []
         for j in range(EB):
-            t = keep.tile([P, T], F32, name=f"v_pool{j}", align_bytes=64)
+            t = stage.tile([P, T], F32, name=f"v_pool{j}", offset=(1 + j) * T * 4)
             nc.sync.dma_start(t[:], vT[j * P : (j + 1) * P, :])
             v_pool.append(t)
 
-        us_cols = keep.tile([P, PACK], F32, name="us_cols")
-        nc.gpsimd.dma_start(us_cols[:], us[0].rearrange("(p t) o -> p (t o)", t=PACK))
-        rw_rows = keep.tile([P, P], F32, name="rw_rows")
+        ident = sb([P, P], F32, "ident")
+        make_identity(nc, ident[:])
+        rw_rows = sb([P, P], F32, "rw_rows")
         nc.gpsimd.memset(rw_rows[:], 0.0)
         nc.gpsimd.dma_start(rw_rows[0:CH, :], rw[0].rearrange("(c p) o -> c (p o)", p=P))
-        ident = keep.tile([P, P], F32, name="ident")
-        make_identity(nc, ident[:])
 
-        warm_in = keep.tile([P, 1], F32, name="warm_in")
-        warm_out = keep.tile([P, 1], F32, name="warm_out")
-        nc.vector.memset(warm_in[:], 0.0)
-        nc.scalar.activation(warm_out[:], warm_in[:], ACT.Silu)
-
-        rw_turned = psum.tile([P, 2, P], F32, name="rw_turned", tag="turn", bufs=2)
-        nc.tensor.transpose(rw_turned[:, 0, :], rw_rows[:], ident[:])
-        rw_cols = keep.tile([P, CH], F32, name="rw_cols")
-        nc.scalar.copy(rw_cols[:], rw_turned[:, 0, 0:CH])
-
-        ks_listed = keep.tile([P, SLOTS], U8, name="ks_listed", align_bytes=64)
-        nc.vector.tensor_copy(ks_listed[:], ks_pool[:].indirect(offsets[:]))
-        k_codes = keep.tile([P, PACK, P], U32, name="k_codes", align_bytes=64)
+        k_codes = sb([P, PACK, P], U32, "k_codes")
         nc.vector.tensor_copy(
             k_codes[:].rearrange("p t s -> p s t"), kw_pool[:].bitcast(U32).indirect(offsets[:])
         )
-        k_scale = keep.tile([P, PACK, P], U8, name="k_scale", align_bytes=64)
+        ks_listed = sb([P, SLOTS], U8, "ks_listed")
+        nc.vector.tensor_copy(ks_listed[:], ks_pool[:].indirect(offsets[:]))
+        k_scale = sb([P, PACK, P], U8, "k_scale")
         nc.vector.tensor_copy(k_scale[:], ks_listed[:].rearrange("p (s t) -> p t s", t=PACK))
 
-        q_codes, q_scale = [], []
+        q_mx = []
         for h in range(2):
-            grouped = keep.tile([P, HALF, PACK], BF16, name=f"q_grouped{h}", align_bytes=64)
-            dst = grouped[:].rearrange("p (c i) t -> p c t i", i=4)
-            src = q_raw[h][:].rearrange("p t (c i) -> p c t i", i=4)
-            if h == 0:
-                nc.vector.tensor_copy(dst, src)
-            else:
-                nc.scalar.copy(dst, src)
-            codes = keep.tile([P, HALF], U32, name=f"q_codes{h}", align_bytes=64)
-            scale = keep.tile([P, HALF], U8, name=f"q_scale{h}", align_bytes=64)
-            nc.vector.quantize_mx(
-                out=codes[:].bitcast(FP8X4), scales=scale[:], in_=grouped[:].rearrange("p w t -> p (w t)")
+            grouped = sb([P, HALF, PACK], BF16, f"q_grouped{h}")
+            nc.scalar.copy(
+                grouped[:].rearrange("p (c i) t -> p c t i", i=4), q_raw[h][:].rearrange("p t (c i) -> p c t i", i=4)
             )
-            q_codes.append(codes)
-            q_scale.append(scale)
+            q_mx.append(quantise(grouped, HALF, f"q{h}"))
 
-        us_wide = us_cols[:].unsqueeze(1).to_broadcast([P, P, PACK])
-        y_codes, y_scale, y_grouped = [], [], []
+        rw_turned = psum.tile([P, P], F32, name="rw_turned", tag="turn", bufs=2)
+        nc.tensor.transpose(rw_turned[:], rw_rows[:], ident[:])
+        rw_cols = sb([P, CH], F32, "rw_cols")
+        nc.scalar.copy(rw_cols[:], rw_turned[:, 0:CH])
 
-        def quantise_y(c):
-            codes = keep.tile([P, P], U32, name=f"y_codes{c}", align_bytes=64)
-            scale = keep.tile([P, P], U8, name=f"y_scale{c}", align_bytes=64)
-            nc.vector.quantize_mx(
-                out=codes[:].bitcast(FP8X4), scales=scale[:], in_=y_grouped[c][:].rearrange("p w t -> p (w t)")
-            )
-            y_codes.append(codes)
-            y_scale.append(scale)
+        v_grouped, v_mx, y_grouped, y_mx = [], [], [], []
 
-        for c in range(CH):
-            h, cols = c // 2, slice((c % 2) * P, (c % 2 + 1) * P)
-            a = psum.tile([P, PACK, P], F32, name="a", tag="a", bufs=2)
-            for t in range(PACK):
-                nc.tensor.matmul_mx(
-                    out=a[:, t, :],
-                    lhsT=k_codes[:, t, :].bitcast(FP8X4),
-                    lhsT_scale=k_scale[:, t, :],
-                    rhs=q_codes[h][:, cols].bitcast(FP8X4),
-                    rhs_scale=q_scale[h][:, cols],
-                    start=True,
-                    stop=True,
-                )
-            act = keep.tile([P, P, PACK], F32, name=f"act{c}")
-            nc.scalar.activation(act[:], a[:].rearrange("p t q -> p q t"), ACT.Silu)
-            grouped = keep.tile([P, P, PACK], BF16, name=f"y_grouped{c}", align_bytes=64)
-            nc.vector.tensor_tensor(grouped[:], act[:], us_wide, MULT)
-            y_grouped.append(grouped)
-            if c > 0:
-                quantise_y(c - 1)
-        quantise_y(CH - 1)
-
-        out_rows = out[0].rearrange("(c p) e -> p c e", p=P)
-        for j in range(EB):
-            listed = keep.tile([P, SLOTS], BF16, name=f"v_listed{j}", align_bytes=64)
+        def turn_v(j, tag):
+            listed = sb([P, SLOTS], BF16, f"v_listed{j}", tag)
             nc.vector.tensor_copy(listed[:], v_pool[j][:].indirect(offsets[:]))
             words = listed[:].bitcast(F32)
             turned = psum.tile([P, 2, P], F32, name="v_turned", tag="turn", bufs=2)
             for u in range(2):
                 nc.tensor.transpose(turned[:, u, :], words[:, u : 2 * P : 2], ident[:])
-            grouped = keep.tile([P, P, PACK], BF16, name=f"v_grouped{j}", align_bytes=64)
+            grouped = sb([P, P, PACK], BF16, f"v_grouped{j}")
             nc.scalar.copy(grouped[:].bitcast(F32), turned[:].rearrange("p u e -> p e u"))
-            codes = keep.tile([P, P], U32, name=f"v_codes{j}", align_bytes=64)
-            scale = keep.tile([P, P], U8, name=f"v_scale{j}", align_bytes=64)
-            nc.vector.quantize_mx(
-                out=codes[:].bitcast(FP8X4), scales=scale[:], in_=grouped[:].rearrange("p w t -> p (w t)")
-            )
-            parts = [range(CH)] if j < EB - 1 else [range(0, 2), range(2, CH)]
-            for part in parts:
-                n = len(part)
-                o = psum.tile([P, n, P], F32, name="o", tag="o", bufs=4)
-                res = keep.tile([P, n, P], F32, name=f"res{j}_{part.start}")
+            v_grouped.append(grouped)
+
+        us_wide = us_cols[:].unsqueeze(1).to_broadcast([P, P, PACK])
+        for c in range(CH):
+            codes, scale = q_mx[c // 2]
+            cols = slice((c % 2) * P, (c % 2 + 1) * P)
+            a = psum.tile([P, PACK, P], F32, name="a", tag="a", bufs=2)
+            for t in range(PACK):
+                product(a[:, t, :], k_codes[:, t, :], k_scale[:, t, :], codes[:, cols], scale[:, cols])
+            act = sb([P, P, PACK], F32, f"act{c}")
+            nc.scalar.activation(act[:], a[:].rearrange("p t q -> p q t"), ACT.Silu)
+            grouped = sb([P, P, PACK], BF16, f"y_grouped{c}")
+            nc.vector.tensor_tensor(grouped[:], act[:], us_wide, MULT)
+            y_grouped.append(grouped)
+            if c > 0:
+                y_mx.append(quantise(y_grouped[c - 1], P, f"y{c - 1}"))
+            if c == 1:
+                turn_v(0, "y_grouped0")
+        v_mx.append(quantise(v_grouped[0], P, "v0"))
+        y_mx.append(quantise(y_grouped[CH - 1], P, f"y{CH - 1}"))
+
+        out_rows = out[0].rearrange("(c p) e -> p c e", p=P)
+
+        def finish(j, part, on_vector, at=None):
+            n = len(part)
+            o = psum.tile([P, n, P], F32, name="o", tag="o", bufs=4)
+            if at is None:
+                res = sb([P, n, P], F32, f"res{j}_{part.start}")
+            else:
+                res = stage.tile([P, n, P], F32, name=f"res{j}", offset=at)
+            for i, c in enumerate(part):
+                product(o[:, i, :], y_mx[c][0][:], y_mx[c][1][:], v_mx[j][0][:], v_mx[j][1][:])
+            if on_vector:
+                rw_wide = rw_cols[:, part.start : part.stop].unsqueeze(2).to_broadcast([P, n, P])
+                nc.vector.tensor_tensor(res[:], o[:], rw_wide, MULT)
+            else:
                 for i, c in enumerate(part):
-                    nc.tensor.matmul_mx(
-                        out=o[:, i, :],
-                        lhsT=y_codes[c][:].bitcast(FP8X4),
-                        lhsT_scale=y_scale[c][:],
-                        rhs=codes[:].bitcast(FP8X4),
-                        rhs_scale=scale[:],
-                        start=True,
-                        stop=True,
-                    )
-                if j == EB - 1 and part.start > 0:
-                    rw_wide = rw_cols[:, part.start : part.stop].unsqueeze(2).to_broadcast([P, n, P])
-                    nc.vector.tensor_tensor(res[:], o[:], rw_wide, MULT)
-                else:
-                    for i, c in enumerate(part):
-                        nc.scalar.activation(res[:, i, :], o[:, i, :], ACT.Copy, scale=rw_cols[:, c : c + 1])
-                nc.sync.dma_start(out_rows[:, part.start : part.stop, j * P : (j + 1) * P], res[:])
+                    nc.scalar.activation(res[:, i, :], o[:, i, :], ACT.Copy, scale=rw_cols[:, c : c + 1])
+            nc.sync.dma_start(out_rows[:, part.start : part.stop, j * P : (j + 1) * P], res[:])
+
+        finish(0, range(CH), False)
+        turn_v(1, "y_grouped3")
+        turn_v(2, None)
+        v_mx.append(quantise(v_grouped[1], P, "v1x", 3 * T * 4))
+        turn_v(3, None)
+        v_mx.append(quantise(v_grouped[2], P, "v2x", 4 * T * 4))
+        finish(1, range(CH), True, 4 * T * 4 + 1024)
+        v_mx.append(quantise(v_grouped[3], P, "v3x"))
+        finish(2, range(CH), True)
+        finish(3, range(0, 2), False)
+        finish(3, range(2, CH), True)

@@ -33,9 +33,9 @@ def tile_attend_mlp_silu_kernel(tc, qT, k_words, k_scales, vT, us, rw, offs, out
         def sb(shape, dtype, name, tag=None):
             return keep.tile(shape, dtype, name=name, tag=tag or name, align_bytes=64)
 
-        def quantise(grouped, width, name, at=None):
+        def quantise(grouped, width, name, at=None, tag=None):
             if at is None:
-                codes = sb([P, width], U32, name + "_codes")
+                codes = sb([P, width], U32, name + "_codes", tag)
             else:
                 codes = stage.tile([P, width], U32, name=name + "_codes", offset=at, align_bytes=64)
             scale = sb([P, width], U8, name + "_scale")
@@ -68,6 +68,9 @@ def tile_attend_mlp_silu_kernel(tc, qT, k_words, k_scales, vT, us, rw, offs, out
                 ks_pool[32 * quad : 32 * quad + 4, :].bitcast(I32),
                 k_scales[0, 4 * quad : 4 * quad + 4, :].bitcast(I32),
             )
+        rw_rows = sb([P, P], F32, "rw_rows")
+        nc.gpsimd.memset(rw_rows[:], 0.0)
+        nc.sync.dma_start(rw_rows[0:CH, :], rw[0].rearrange("(c p) o -> c (p o)", p=P))
         warm_in = stage.tile([P, (1 + EB) * T], F32, name="warm_in", offset=0)
         warm_out = sb([P, 1], F32, "warm_out")
         nc.gpsimd.memset(warm_in[:, 0:1], 0.0)
@@ -88,9 +91,6 @@ def tile_attend_mlp_silu_kernel(tc, qT, k_words, k_scales, vT, us, rw, offs, out
 
         ident = sb([P, P], F32, "ident")
         make_identity(nc, ident[:])
-        rw_rows = sb([P, P], F32, "rw_rows")
-        nc.gpsimd.memset(rw_rows[:], 0.0)
-        nc.gpsimd.dma_start(rw_rows[0:CH, :], rw[0].rearrange("(c p) o -> c (p o)", p=P))
 
         k_codes = sb([P, PACK, P], U32, "k_codes")
         nc.vector.tensor_copy(
@@ -98,8 +98,6 @@ def tile_attend_mlp_silu_kernel(tc, qT, k_words, k_scales, vT, us, rw, offs, out
         )
         ks_listed = sb([P, SLOTS], U8, "ks_listed")
         nc.vector.tensor_copy(ks_listed[:], ks_pool[:].indirect(offsets[:]))
-        k_scale = sb([P, PACK, P], U8, "k_scale")
-        nc.vector.tensor_copy(k_scale[:], ks_listed[:].rearrange("p (s t) -> p t s", t=PACK))
 
         q_mx = []
         for h in range(2):
@@ -108,13 +106,16 @@ def tile_attend_mlp_silu_kernel(tc, qT, k_words, k_scales, vT, us, rw, offs, out
                 grouped[:].rearrange("p (c i) t -> p c t i", i=4), q_raw[h][:].rearrange("p t (c i) -> p c t i", i=4)
             )
             q_mx.append(quantise(grouped, HALF, f"q{h}"))
+            if h == 0:
+                k_scale = sb([P, PACK, P], U8, "k_scale", "q_grouped0")
+                nc.vector.tensor_copy(k_scale[:], ks_listed[:].rearrange("p (s t) -> p t s", t=PACK))
 
         rw_turned = psum.tile([P, P], F32, name="rw_turned", tag="turn", bufs=2)
         nc.tensor.transpose(rw_turned[:], rw_rows[:], ident[:])
         rw_cols = sb([P, CH], F32, "rw_cols")
         nc.scalar.copy(rw_cols[:], rw_turned[:, 0:CH])
 
-        v_grouped, v_mx, y_grouped, y_mx = [], [], [], []
+        v_grouped, v_mx, y_mx = [], [], []
 
         def turn_v(j, tag):
             listed = sb([P, SLOTS], BF16, f"v_listed{j}", tag)
@@ -127,7 +128,12 @@ def tile_attend_mlp_silu_kernel(tc, qT, k_words, k_scales, vT, us, rw, offs, out
             nc.scalar.copy(grouped[:].bitcast(F32), turned[:].rearrange("p u e -> p e u"))
             v_grouped.append(grouped)
 
+        turn_v(0, None)
         us_wide = us_cols[:].unsqueeze(1).to_broadcast([P, P, PACK])
+        y_grouped = [
+            stage.tile([P, HALF, PACK], BF16, name="y_grouped0", offset=T * 4, align_bytes=64),
+            sb([P, HALF, PACK], BF16, "y_grouped1"),
+        ]
         for c in range(CH):
             codes, scale = q_mx[c // 2]
             cols = slice((c % 2) * P, (c % 2 + 1) * P)
@@ -136,27 +142,21 @@ def tile_attend_mlp_silu_kernel(tc, qT, k_words, k_scales, vT, us, rw, offs, out
                 product(a[:, t, :], k_codes[:, t, :], k_scale[:, t, :], codes[:, cols], scale[:, cols])
             act = sb([P, P, PACK], F32, f"act{c}")
             nc.scalar.activation(act[:], a[:].rearrange("p t q -> p q t"), ACT.Silu)
-            grouped = sb([P, P, PACK], BF16, f"y_grouped{c}")
-            nc.vector.tensor_tensor(grouped[:], act[:], us_wide, MULT)
-            y_grouped.append(grouped)
-            if c > 0:
-                y_mx.append(quantise(y_grouped[c - 1], P, f"y{c - 1}"))
-            if c == 1:
-                turn_v(0, "y_grouped0")
-        v_mx.append(quantise(v_grouped[0], P, "v0"))
-        y_mx.append(quantise(y_grouped[CH - 1], P, f"y{CH - 1}"))
+            nc.vector.tensor_tensor(y_grouped[c // 2][:, cols, :], act[:], us_wide, MULT)
+            if c == 2:
+                y_mx.append(quantise(y_grouped[0], HALF, "y0", tag="act2"))
+        v_mx.append(quantise(v_grouped[0], P, "v0x", tag="act3"))
+        y_mx.append(quantise(y_grouped[1], HALF, "y1"))
 
         out_rows = out[0].rearrange("(c p) e -> p c e", p=P)
 
-        def finish(j, part, on_vector, at=None):
+        def finish(j, part, on_vector, tag=None):
             n = len(part)
             o = psum.tile([P, n, P], F32, name="o", tag="o", bufs=4)
-            if at is None:
-                res = sb([P, n, P], F32, f"res{j}_{part.start}")
-            else:
-                res = stage.tile([P, n, P], F32, name=f"res{j}", offset=at)
+            res = sb([P, n, P], F32, f"res{j}_{part.start}", tag)
             for i, c in enumerate(part):
-                product(o[:, i, :], y_mx[c][0][:], y_mx[c][1][:], v_mx[j][0][:], v_mx[j][1][:])
+                cols = slice((c % 2) * P, (c % 2 + 1) * P)
+                product(o[:, i, :], y_mx[c // 2][0][:, cols], y_mx[c // 2][1][:, cols], v_mx[j][0][:], v_mx[j][1][:])
             if on_vector:
                 rw_wide = rw_cols[:, part.start : part.stop].unsqueeze(2).to_broadcast([P, n, P])
                 nc.vector.tensor_tensor(res[:], o[:], rw_wide, MULT)
@@ -166,13 +166,13 @@ def tile_attend_mlp_silu_kernel(tc, qT, k_words, k_scales, vT, us, rw, offs, out
             nc.sync.dma_start(out_rows[:, part.start : part.stop, j * P : (j + 1) * P], res[:])
 
         finish(0, range(CH), False)
-        turn_v(1, "y_grouped3")
+        turn_v(1, None)
         turn_v(2, None)
         v_mx.append(quantise(v_grouped[1], P, "v1x", 3 * T * 4))
+        finish(1, range(CH), False)
         turn_v(3, None)
         v_mx.append(quantise(v_grouped[2], P, "v2x", 4 * T * 4))
-        finish(1, range(CH), True, 4 * T * 4 + 1024)
         v_mx.append(quantise(v_grouped[3], P, "v3x"))
-        finish(2, range(CH), True)
+        finish(2, range(CH), True, "v_grouped3")
         finish(3, range(0, 2), False)
         finish(3, range(2, CH), True)

from contextlib import ExitStack

import concourse.mybir as mybir
from concourse.masks import make_identity

D, NQ, T, SLOTS, DV = 512, 512, 2048, 512, 512
FLOPS = 2 * SLOTS * NQ * D + 2 * NQ * SLOTS * DV

F32 = mybir.dt.float32
BF16 = mybir.dt.bfloat16
I32 = mybir.dt.int32
U32 = mybir.dt.uint32
U16 = mybir.dt.uint16
U8 = mybir.dt.uint8
FP8X4 = mybir.dt.float8_e4m3fn_x4
ACT = mybir.ActivationFunctionType
MULT = mybir.AluOpType.mult

P = 128
PACK = 4
CH = NQ // P
EB = DV // P
HALF = NQ // 2


def tile_attend_mlp_silu_kernel(tc, qT, k_words, k_scales, vT, us, rw, offs, out):
    nc = tc.nc
    with ExitStack() as ctx:
        keep = ctx.enter_context(tc.tile_pool(name="keep", bufs=1))
        stage = ctx.enter_context(tc.tile_pool(name="stage", bufs=1))
        psum = ctx.enter_context(tc.psum_pool(name="psum", bufs=1))

        def sb(shape, dtype, name, tag=None):
            return keep.tile(shape, dtype, name=name, tag=tag or name, align_bytes=64)

        def quantise(grouped, width, name, at=None, tag=None):
            if at is None:
                codes = sb([P, width], U32, name + "_codes", tag)
            else:
                codes = stage.tile([P, width], U32, name=name + "_codes", offset=at, align_bytes=64)
            scale = sb([P, width], U8, name + "_scale")
            nc.vector.quantize_mx(
                out=codes[:].bitcast(FP8X4), scales=scale[:], in_=grouped[:].rearrange("p w t -> p (w t)")
            )
            return codes, scale

        def product(dst, stat, stat_scale, mov, mov_scale):
            nc.tensor.matmul_mx(
                out=dst,
                lhsT=stat.bitcast(FP8X4),
                lhsT_scale=stat_scale,
                rhs=mov.bitcast(FP8X4),
                rhs_scale=mov_scale,
                start=True,
                stop=True,
            )

        offsets = keep.tile([P, SLOTS // 16], U16, name="offsets")
        nc.sync.dma_start(offsets[:], offs)
        us_cols = sb([P, PACK], F32, "us_cols")
        nc.scalar.dma_start(us_cols[:], us[0].rearrange("(p t) o -> p (t o)", t=PACK))
        kw_pool = sb([P, T], I32, "kw_pool")
        nc.sync.dma_start(kw_pool[:], k_words[0].rearrange("p n t -> p (n t)").bitcast(I32))
        ks_pool = sb([P, T], U8, "ks_pool")
        nc.gpsimd.memset(ks_pool[:].bitcast(I32), 0)
        for quad in range(4):
            nc.sync.dma_start(
                ks_pool[32 * quad : 32 * quad + 4, :].bitcast(I32),
                k_scales[0, 4 * quad : 4 * quad + 4, :].bitcast(I32),
            )
        rw_rows = sb([P, P], F32, "rw_rows")
        nc.gpsimd.memset(rw_rows[:], 0.0)
        nc.sync.dma_start(rw_rows[0:CH, :], rw[0].rearrange("(c p) o -> c (p o)", p=P))
        warm_in = stage.tile([P, (1 + EB) * T], F32, name="warm_in", offset=0)
        warm_out = sb([P, 1], F32, "warm_out")
        nc.gpsimd.memset(warm_in[:, 0:1], 0.0)
        nc.scalar.activation(warm_out[:], warm_in[:, 0:1], ACT.Silu)

        q_rows = qT[0].rearrange("(p j) q -> p j q", j=PACK)
        q_raw = []
        for h in range(2):
            t = stage.tile([P, PACK, HALF], F32, name=f"q_raw{h}", offset=h * T * 2)
            nc.sync.dma_start(t[:], q_rows[:, :, h * HALF : (h + 1) * HALF])
            q_raw.append(t)

        v_pool = []
        for j in range(EB):
            t = stage.tile([P, T], F32, name=f"v_pool{j}", offset=(1 + j) * T * 4)
            nc.sync.dma_start(t[:], vT[j * P : (j + 1) * P, :])
            v_pool.append(t)

        ident = sb([P, P], F32, "ident")
        make_identity(nc, ident[:])

        k_codes = sb([P, PACK, P], U32, "k_codes")
        nc.vector.tensor_copy(
            k_codes[:].rearrange("p t s -> p s t"), kw_pool[:].bitcast(U32).indirect(offsets[:])
        )
        ks_listed = sb([P, SLOTS], U8, "ks_listed")
        nc.vector.tensor_copy(ks_listed[:], ks_pool[:].indirect(offsets[:]))

        q_mx = []
        for h in range(2):
            grouped = sb([P, HALF, PACK], BF16, f"q_grouped{h}")
            nc.scalar.copy(
                grouped[:].rearrange("p (c i) t -> p c t i", i=4), q_raw[h][:].rearrange("p t (c i) -> p c t i", i=4)
            )
            q_mx.append(quantise(grouped, HALF, f"q{h}"))
            if h == 0:
                k_scale = sb([P, PACK, P], U8, "k_scale", "q_grouped0")
                nc.vector.tensor_copy(k_scale[:], ks_listed[:].rearrange("p (s t) -> p t s", t=PACK))

        rw_turned = psum.tile([P, P], F32, name="rw_turned", tag="turn", bufs=2)
        nc.tensor.transpose(rw_turned[:], rw_rows[:], ident[:])
        rw_cols = sb([P, CH], F32, "rw_cols")
        nc.scalar.copy(rw_cols[:], rw_turned[:, 0:CH])

        v_grouped, v_mx, y_mx = [], [], []

        def turn_v(j, tag):
            listed = sb([P, SLOTS], BF16, f"v_listed{j}", tag)
            nc.vector.tensor_copy(listed[:], v_pool[j][:].indirect(offsets[:]))
            words = listed[:].bitcast(F32)
            turned = psum.tile([P, 2, P], F32, name="v_turned", tag="turn", bufs=2)
            for u in range(2):
                nc.tensor.transpose(turned[:, u, :], words[:, u : 2 * P : 2], ident[:])
            grouped = sb([P, P, PACK], BF16, f"v_grouped{j}")
            nc.scalar.copy(grouped[:].bitcast(F32), turned[:].rearrange("p u e -> p e u"))
            v_grouped.append(grouped)

        turn_v(0, None)
        us_wide = us_cols[:].unsqueeze(1).to_broadcast([P, P, PACK])
        y_grouped = [
            stage.tile([P, HALF, PACK], BF16, name="y_grouped0", offset=T * 4, align_bytes=64),
            sb([P, HALF, PACK], BF16, "y_grouped1"),
        ]
        for c in range(CH):
            codes, scale = q_mx[c // 2]
            cols = slice((c % 2) * P, (c % 2 + 1) * P)
            a = psum.tile([P, PACK, P], F32, name="a", tag="a", bufs=2)
            for t in range(PACK):
                product(a[:, t, :], k_codes[:, t, :], k_scale[:, t, :], codes[:, cols], scale[:, cols])
            act = sb([P, P, PACK], F32, f"act{c}")
            nc.scalar.activation(act[:], a[:].rearrange("p t q -> p q t"), ACT.Silu)
            nc.vector.tensor_tensor(y_grouped[c // 2][:, cols, :], act[:], us_wide, MULT)
            if c == 2:
                y_mx.append(quantise(y_grouped[0], HALF, "y0", tag="act2"))
        v_mx.append(quantise(v_grouped[0], P, "v0x", tag="act3"))
        y_mx.append(quantise(y_grouped[1], HALF, "y1"))

        out_rows = out[0].rearrange("(c p) e -> p c e", p=P)

        def finish(j, part, on_vector, tag=None):
            n = len(part)
            o = psum.tile([P, n, P], F32, name="o", tag="o", bufs=4)
            res = sb([P, n, P], F32, f"res{j}_{part.start}", tag)
            for i, c in enumerate(part):
                cols = slice((c % 2) * P, (c % 2 + 1) * P)
                product(o[:, i, :], y_mx[c // 2][0][:, cols], y_mx[c // 2][1][:, cols], v_mx[j][0][:], v_mx[j][1][:])
            if on_vector:
                rw_wide = rw_cols[:, part.start : part.stop].unsqueeze(2).to_broadcast([P, n, P])
                nc.vector.tensor_tensor(res[:], o[:], rw_wide, MULT)
            else:
                for i, c in enumerate(part):
                    nc.scalar.activation(res[:, i, :], o[:, i, :], ACT.Copy, scale=rw_cols[:, c : c + 1])
            nc.sync.dma_start(out_rows[:, part.start : part.stop, j * P : (j + 1) * P], res[:])

        finish(0, range(CH), False)
        turn_v(1, None)
        turn_v(2, None)
        v_mx.append(quantise(v_grouped[1], P, "v1x", 3 * T * 4))
        finish(1, range(CH), False)
        turn_v(3, None)
        v_mx.append(quantise(v_grouped[2], P, "v2x", 4 * T * 4))
        v_mx.append(quantise(v_grouped[3], P, "v3x"))
        finish(2, range(CH), True, "v_grouped3")
        finish(3, range(0, 2), False)
        finish(3, range(2, CH), True)
